import numpy as np
import ml_dtypes


def mxq(x, axis, fmt="e4m3"):
    dtype, down = {"e4m3": (ml_dtypes.float8_e4m3fn, 7), "e5m2": (ml_dtypes.float8_e5m2, 14)}[fmt]
    v = np.moveaxis(np.asarray(x, np.float32).astype(ml_dtypes.bfloat16).astype(np.float64), axis, -1)
    blocks = v.reshape(v.shape[:-1] + (-1, 32))
    amax = np.abs(blocks).max(-1, keepdims=True)
    byte = np.maximum(np.where(amax > 0, np.frexp(amax)[1] - 1 + 127, 0) - down, 1)
    scale = np.exp2(byte - 127.0)
    codes = (blocks / scale).astype(np.float32).astype(dtype).astype(np.float64)
    return np.moveaxis((codes * scale).reshape(v.shape), -1, axis)


WIDE = False


def mx_kscale(k):
    if not WIDE:
        return np.ones(k)
    levels = np.array([30, -30])
    if k % 512:
        return np.exp2(np.random.permutation(np.resize(levels, k // 32))).repeat(32)
    a = np.empty((k // 512, 16))
    for p in range(k // 512):
        a[p, :8] = np.random.permutation(np.resize(levels, 8))
        for g in range(8):
            far = levels[np.abs(levels - a[p, g]) >= 10]
            a[p, g + 8] = far[np.random.randint(len(far))]
    return np.exp2(a.ravel()).repeat(32)


def f64(x):
    return np.asarray(x).astype(np.float64)


def striped(idx):
    return np.tile(np.asarray(idx).reshape(-1, 16).T, (8, 1)).astype(np.uint16)


def unstriped(offs):
    return offs[:16].T.reshape(-1).astype(np.int64)


E2M1 = np.array([0.0, 0.5, 1.0, 1.5, 2.0, 3.0, 4.0, 6.0, -0.0, -0.5, -1.0, -1.5, -2.0, -3.0, -4.0, -6.0])


def pack_weight(w, fmt):
    k, n = w.shape
    w = f64(np.asarray(w, np.float32).astype(ml_dtypes.bfloat16)).reshape(k // 32, 32, n)
    amax = np.abs(w).max(1)
    if fmt in ("e4m3", "e5m2"):
        byte = np.frexp(amax)[1] - 1 + 127 - (7 if fmt == "e4m3" else 14)
    else:
        mant, ex = np.frexp(amax / 6.0)
        byte = np.where(mant > 0.5, ex, ex - 1) + 127
    byte = np.clip(np.where(amax > 0, byte, 1), 1, 254)
    scaled = (w * np.exp2(127.0 - byte)[:, None, :]).reshape(k, n).astype(np.float32)
    by_word = np.ascontiguousarray(scaled.reshape(k // 512, 128, 4, n).transpose(0, 1, 3, 2))
    if fmt in ("e4m3", "e5m2"):
        words = by_word.astype(ml_dtypes.float8_e4m3fn if fmt == "e4m3" else ml_dtypes.float8_e5m2).view(np.uint8)
    else:
        c = by_word.astype(ml_dtypes.float4_e2m1fn).view(np.uint8) & 0xF
        words = (c[..., 0::2] | (c[..., 1::2] << 4)).reshape(k // 512, 128, 2 * n)
    return np.ascontiguousarray(words), np.ascontiguousarray(byte.astype(np.uint8).reshape(k // 512, 16, n))


def unpack_weight(words, scales, fmt):
    g, _, n = scales.shape
    words = np.ascontiguousarray(words).reshape(g, 128, n, -1)
    if fmt in ("e4m3", "e5m2"):
        vals = words.view(ml_dtypes.float8_e4m3fn if fmt == "e4m3" else ml_dtypes.float8_e5m2).astype(np.float64)
    else:
        nib = np.empty((g, 128, n, 4), np.uint8)
        nib[..., 0::2] = words & 0xF
        nib[..., 1::2] = words >> 4
        vals = E2M1[nib]
    vals = vals * np.repeat(np.exp2(scales.astype(np.float64) - 127.0), 8, axis=1)[..., None]
    return vals.transpose(0, 1, 3, 2).reshape(g * 512, n)


def sigmoid(v):
    return 1.0 / (1.0 + np.exp(-v))


def sgn(shape):
    return np.random.uniform(0.5, 2.0, shape) * np.where(np.random.standard_normal(shape) < 0, -1.0, 1.0)


K, T, J, R, V, X, O, N, U, E = 512, 1024, 256, 512, 1024, 1024, 256, 256, 128, 512


def setup_inputs():
    n = np.random.standard_normal
    idx = np.random.permutation(V)[:R]
    idx2 = np.random.permutation(T)[:J]
    idx3 = np.random.permutation(X)[:O]
    idx4 = np.random.permutation(X)[:O]
    idx5 = np.random.permutation(J)[:O]
    idx6 = np.random.permutation(O)[:U]
    idx7 = np.random.permutation(E)[:U]
    fk = mx_kscale(K)
    fr = mx_kscale(R)
    xtp = pack_weight(n((K, T)) / fk[:, None], "e4m3")
    wtp = pack_weight(n((K, V)) * 1 / np.sqrt(K) * fk[:, None], "e2m1")
    wbp = pack_weight(n((R, N)) * 1 / np.sqrt(R) / fr[:, None], "e5m2")
    return {
        "xt_words": xtp[0],
        "xt_scales": xtp[1],
        "wt_words": wtp[0],
        "wt_scales": wtp[1],
        "tb": (np.random.randint(-7, 8, (R, X)).astype(np.float64)).astype(np.float32),
        "st": (np.random.uniform(0.15, 0.35, (R, 1)) * fr[:, None]).astype(np.float32),
        "sa": (np.random.uniform(0.5, 1.6, (R, 1)) * fr[:, None]).astype(np.float32),
        "sg": (0.3 * sgn((R, 1))).astype(np.float32),
        "bg": (np.random.uniform(-2.0, 2.0, (R, 1))).astype(np.float32),
        "wb_words": wbp[0],
        "wb_scales": wbp[1],
        "so": (sgn((N, 1))).astype(np.float32),
        "offs": striped(idx),
        "offs2": striped(idx2),
        "offs3": striped(idx3),
        "offs4": striped(idx4),
        "offs5": striped(idx5),
        "offs6": striped(idx6),
        "offs7": striped(idx7),
    }


def reference(xt_words, xt_scales, wt_words, wt_scales, tb, st, sa, sg, bg, wb_words, wb_scales, so, offs, offs2, offs3, offs4, offs5, offs6, offs7):
    idx = unstriped(offs)
    idx2 = unstriped(offs2)
    idx3 = unstriped(offs3)
    idx4 = unstriped(offs4)
    idx5 = unstriped(offs5)
    idx6 = unstriped(offs6)
    idx7 = unstriped(offs7)
    xtu = unpack_weight(xt_words, xt_scales, "e4m3")
    wtu = unpack_weight(wt_words, wt_scales, "e2m1")
    wbu = unpack_weight(wb_words, wb_scales, "e5m2")
    wtidxg = wtu[:, idx]
    xtidx2g = xtu[:, idx2]
    a = wtidxg.T @ xtidx2g
    u1 = f64(tb)[:, idx3] * f64(st) * sigmoid(f64(tb)[:, idx4] * f64(sg) + f64(bg))
    hid = np.maximum(u1, a[:, idx5] * f64(sa))
    hidq = mxq(hid, 0, "e4m3")
    p = wbu.T @ hidq
    m0 = p[:, idx6] * f64(so)
    y = np.zeros((N, E))
    y[:, idx7] = m0
    return y

@@ -1,0 +1,188 @@
+from contextlib import ExitStack
+
+import concourse.mybir as mybir
+
+K, T, J, R, V, X, O, N, U, E = 512, 1024, 256, 512, 1024, 1024, 256, 256, 128, 512
+FLOPS = 2 * K * R * J + 2 * R * N * O
+
+F32 = mybir.dt.float32
+BF16 = mybir.dt.bfloat16
+I32 = mybir.dt.int32
+U32 = mybir.dt.uint32
+U16 = mybir.dt.uint16
+U8 = mybir.dt.uint8
+E4M3 = mybir.dt.float8_e4m3fn_x4
+E5M2 = mybir.dt.float8_e5m2_x4
+E2M1 = mybir.dt.float4_e2m1fn_x4
+ACT = mybir.ActivationFunctionType
+ALU = mybir.AluOpType
+
+P = 128
+PACK = 4
+QUADRANTS = 4
+QUADRANT = 32
+HALVES = 2
+HALF = O // HALVES
+PER_COLUMN = 16
+
+
+def tile_list_gatedlevels_chosen_one_postedout_kernel(
+    tc, xt_words, xt_scales, wt_words, wt_scales, tb, st, sa, sg, bg, wb_words, wb_scales, so,
+    offs, offs2, offs3, offs4, offs5, offs6, offs7, out,
+):
+    nc = tc.nc
+    with ExitStack() as ctx:
+        sb = ctx.enter_context(tc.tile_pool(name="sb", bufs=1))
+        psum = ctx.enter_context(tc.psum_pool(name="psum", bufs=1))
+
+        def load_list(src, name):
+            tile = sb.tile(list(src.shape), U16, name=name)
+            nc.sync.dma_start(tile[:], src)
+            return tile
+
+        def zeroed_plane(width, name):
+            plane = sb.tile([P, width], U8, name=name, tag=name, align_bytes=64)
+            nc.vector.memset(plane[:].bitcast(I32), 0)
+            return plane
+
+        def load_scale_rows(plane, src):
+            for q in range(QUADRANTS):
+                nc.sync.dma_start(
+                    plane[:].bitcast(I32)[QUADRANT * q : QUADRANT * q + PACK, :],
+                    src[0].bitcast(I32)[PACK * q : PACK * (q + 1), :],
+                )
+
+        def load_per_row(src, name):
+            tile = sb.tile([P, PACK], F32, name=name)
+            nc.gpsimd.dma_start(tile[:], src.rearrange("(p t) one -> p (t one)", t=PACK))
+            return tile
+
+        tb_slots = tb.rearrange("(p t) x -> t p x", t=PACK)
+
+        def load_levels(t):
+            tile = sb.tile([P, X], F32, name=f"levels{t}", tag=f"levels{t}")
+            nc.sync.dma_start(tile[:], tb_slots[t])
+            return tile
+
+        wt_plane = zeroed_plane(V, "wt_plane")
+        xt_plane = zeroed_plane(T, "xt_plane")
+        wb_plane = zeroed_plane(N, "wb_plane")
+        pages = []
+        for h in range(HALVES):
+            page = sb.tile([P, E], F32, name=f"page{h}")
+            nc.vector.memset(page[:], 0.0)
+            pages.append(page)
+
+        sg_sb = load_per_row(sg, "sg_sb")
+        bg_sb = load_per_row(bg, "bg_sb")
+        st_sb = load_per_row(st, "st_sb")
+        sa_sb = load_per_row(sa, "sa_sb")
+        so_sb = sb.tile([P, HALVES], F32, name="so_sb")
+        with nc.allow_non_contiguous_dma(reason="one weight for each partition and half of the output features"):
+            nc.gpsimd.dma_start(so_sb[:], so.rearrange("(h p) one -> p (h one)", p=P))
+
+        wt_list = load_list(offs, "wt_list")
+        wt_all = sb.tile([P, V], U16, name="wt_all")
+        nc.sync.dma_start(wt_all[:].bitcast(I32), wt_words[0].bitcast(I32))
+        load_scale_rows(wt_plane, wt_scales)
+        gate_list = load_list(offs4, "gate_list")
+        levels = [load_levels(0)]
+        step_list = load_list(offs3, "step_list")
+        xt_all = sb.tile([P, T], U32, name="xt_all")
+        nc.sync.dma_start(xt_all[:].bitcast(I32), xt_words[0].rearrange("p c t -> p (c t)").bitcast(I32))
+        xt_list = load_list(offs2, "xt_list")
+        load_scale_rows(xt_plane, xt_scales)
+        levels.extend(load_levels(t) for t in (1, 2))
+        slot_list = load_list(offs5, "slot_list")
+        levels.append(load_levels(3))
+        wb_codes = sb.tile([P, N], U32, name="wb_codes", align_bytes=64)
+        nc.sync.dma_start(wb_codes[:].bitcast(I32), wb_words[0].rearrange("p c t -> p (c t)").bitcast(I32))
+        load_scale_rows(wb_plane, wb_scales)
+        place_list = load_list(offs6, "place_list")
+        page_list = load_list(offs7, "page_list")
+
+        wt_picked = sb.tile([P, R], U16, name="wt_picked")
+        nc.vector.tensor_copy(wt_picked[:], wt_all[:].indirect(wt_list[:]))
+        wt_codes = sb.tile([P, PACK, P], U16, name="wt_codes", align_bytes=64)
+        nc.vector.tensor_copy(
+            wt_codes[:].rearrange("p t (c i) -> p c t i", i=8),
+            wt_picked[:].rearrange("p (c i t) -> p c t i", i=8, t=PACK),
+        )
+        wt_scale = sb.tile([P, PACK, P], U8, name="wt_scale", align_bytes=64)
+        nc.vector.tensor_copy(wt_scale[:].rearrange("p t m -> p m t"), wt_plane[:].indirect(wt_list[:]))
+        xt_codes = sb.tile([P, J], U32, name="xt_codes", align_bytes=64)
+        nc.vector.tensor_copy(xt_codes[:], xt_all[:].indirect(xt_list[:]))
+        xt_scale = sb.tile([P, J], U8, name="xt_scale", align_bytes=64)
+        nc.vector.tensor_copy(xt_scale[:], xt_plane[:].indirect(xt_list[:]))
+
+        a_rows = []
+        for t in range(PACK):
+            bank = psum.tile([P, J], F32, name=f"a_bank{t}")
+            nc.tensor.matmul_mx(
+                out=bank[:], lhsT=wt_codes[:, t, :].bitcast(E2M1), lhsT_scale=wt_scale[:, t, :],
+                rhs=xt_codes[:].bitcast(E4M3), rhs_scale=xt_scale[:], start=True, stop=True,
+            )
+            rows = sb.tile([P, J], F32, name=f"a_rows{t}")
+            nc.vector.tensor_copy(rows[:], bank[:])
+            a_rows.append(rows)
+
+        u1 = []
+        for t in range(PACK):
+            gate = sb.tile([P, O], F32, name=f"gate{t}")
+            nc.scalar.activation(
+                gate[:], levels[t][:].indirect(gate_list[:]), ACT.Sigmoid,
+                bias=bg_sb[:, t : t + 1], scale=sg_sb[:, t : t + 1],
+            )
+            stepped = sb.tile([P, O], F32, name=f"stepped{t}")
+            nc.scalar.activation(
+                stepped[:], levels[t][:].indirect(step_list[:]), ACT.Copy, scale=st_sb[:, t : t + 1],
+            )
+            gated = sb.tile([P, O], F32, name=f"gated{t}", tag="xt_plane" if t == 0 else f"gated{t}", align_bytes=64)
+            nc.vector.tensor_tensor(gated[:], stepped[:], gate[:], ALU.mult)
+            u1.append(gated)
+
+        p_rows = [sb.tile([P, O], F32, name=f"p_rows{h}") for h in range(HALVES)]
+        chosen = sb.tile([P, HALVES, PACK, HALF], F32, name="chosen", tag=f"levels{PACK - 1}")
+        for half in range(HALVES):
+            places = slice(half * HALF, (half + 1) * HALF)
+            columns = slice(half * HALF // PER_COLUMN, (half + 1) * HALF // PER_COLUMN)
+            hid = sb.tile([P, PACK, HALF], BF16, name="hid")
+            for t in range(PACK):
+                nc.scalar.activation(
+                    chosen[:, half, t, :], a_rows[t][:].indirect(slot_list[:, columns]), ACT.Copy,
+                    scale=sa_sb[:, t : t + 1],
+                )
+                nc.vector.tensor_tensor(hid[:, t, :], u1[t][:, places], chosen[:, half, t, :], ALU.max)
+            woven = sb.tile([P, HALF, PACK], BF16, name=f"woven{half}", align_bytes=64)
+            nc.vector.tensor_copy(
+                woven[:].rearrange("p (c i) t -> p c t i", i=4),
+                hid[:].rearrange("p t (c i) -> p c t i", i=4),
+            )
+            hid_codes = sb.tile([P, HALF], U32, name=f"hid_codes{half}", align_bytes=64)
+            hid_scale = sb.tile([P, HALF], U8, name=f"hid_scale{half}", align_bytes=64)
+            nc.vector.quantize_mx(
+                out=hid_codes[:].bitcast(E4M3), scales=hid_scale[:], in_=woven[:].rearrange("p o t -> p (o t)"),
+            )
+            for h in range(HALVES):
+                features = slice(h * P, (h + 1) * P)
+                bank = psum.tile([P, HALF], F32, name=f"p_bank{half}_{h}")
+                nc.tensor.matmul_mx(
+                    out=bank[:], lhsT=wb_codes[:, features].bitcast(E5M2), lhsT_scale=wb_plane[:, features],
+                    rhs=hid_codes[:].bitcast(E4M3), rhs_scale=hid_scale[:], start=True, stop=True,
+                )
+                if half == HALVES - 1 and h == 0:
+                    nc.scalar.copy(p_rows[h][:, places], bank[:])
+                else:
+                    nc.vector.tensor_copy(p_rows[h][:, places], bank[:])
+
+        for h in range(HALVES):
+            ends = sb.tile([P, U], F32, name=f"ends{h}")
+            nc.scalar.activation(
+                ends[:], p_rows[h][:].indirect(place_list[:]), ACT.Copy, scale=so_sb[:, h : h + 1],
+            )
+            if h == 0:
+                nc.vector.tensor_copy(pages[h][:].indirect(page_list[:]), ends[:])
+                nc.sync.dma_start(out[h * P : (h + 1) * P, :], pages[h][:])
+            else:
+                nc.scalar.activation(pages[h][:].indirect(page_list[:]), ends[:], ACT.Copy)
+                nc.scalar.dma_start(out[h * P : (h + 1) * P, :], pages[h][:])

@@ -45,16 +45,19 @@ def tile_list_gatedlevels_chosen_one_postedout_kernel(
             nc.vector.memset(plane[:].bitcast(I32), 0)
             return plane
 
-        def load_scale_rows(plane, src):
+        def load_scale_rows(src, name):
+            width = src.shape[2] // 4
+            rows = sb.tile([PACK, QUADRANTS, width], I32, name=name)
+            nc.sync.dma_start(rows[:], src[0].bitcast(I32).rearrange("(q r) c -> r q c", r=PACK))
+            return rows
+
+        def spread_scale_rows(plane, rows):
             for q in range(QUADRANTS):
-                nc.sync.dma_start(
-                    plane[:].bitcast(I32)[QUADRANT * q : QUADRANT * q + PACK, :],
-                    src[0].bitcast(I32)[PACK * q : PACK * (q + 1), :],
-                )
+                nc.vector.tensor_copy(plane[:].bitcast(I32)[QUADRANT * q : QUADRANT * q + PACK, :], rows[:, q, :])
 
         def load_per_row(src, name):
             tile = sb.tile([P, PACK], F32, name=name)
-            nc.gpsimd.dma_start(tile[:], src.rearrange("(p t) one -> p (t one)", t=PACK))
+            nc.sync.dma_start(tile[:], src.rearrange("(p t) one -> p (t one)", t=PACK))
             return tile
 
         tb_slots = tb.rearrange("(p t) x -> t p x", t=PACK)
@@ -70,37 +73,41 @@ def tile_list_gatedlevels_chosen_one_postedout_kernel(
         pages = []
         for h in range(HALVES):
             page = sb.tile([P, E], F32, name=f"page{h}")
-            nc.vector.memset(page[:], 0.0)
+            nc.gpsimd.memset(page[:], 0.0)
             pages.append(page)
 
-        sg_sb = load_per_row(sg, "sg_sb")
-        bg_sb = load_per_row(bg, "bg_sb")
-        st_sb = load_per_row(st, "st_sb")
-        sa_sb = load_per_row(sa, "sa_sb")
-        so_sb = sb.tile([P, HALVES], F32, name="so_sb")
-        with nc.allow_non_contiguous_dma(reason="one weight for each partition and half of the output features"):
-            nc.gpsimd.dma_start(so_sb[:], so.rearrange("(h p) one -> p (h one)", p=P))
-
         wt_list = load_list(offs, "wt_list")
+        wt_rows = load_scale_rows(wt_scales, "wt_rows")
         wt_all = sb.tile([P, V], U16, name="wt_all")
         nc.sync.dma_start(wt_all[:].bitcast(I32), wt_words[0].bitcast(I32))
-        load_scale_rows(wt_plane, wt_scales)
         gate_list = load_list(offs4, "gate_list")
-        levels = [load_levels(0)]
+        sg_sb = load_per_row(sg, "sg_sb")
+        bg_sb = load_per_row(bg, "bg_sb")
+        levels = [load_levels(t) for t in (0, 1)]
         step_list = load_list(offs3, "step_list")
-        xt_all = sb.tile([P, T], U32, name="xt_all")
-        nc.sync.dma_start(xt_all[:].bitcast(I32), xt_words[0].rearrange("p c t -> p (c t)").bitcast(I32))
+        st_sb = load_per_row(st, "st_sb")
+        xt_rows = load_scale_rows(xt_scales, "xt_rows")
         xt_list = load_list(offs2, "xt_list")
-        load_scale_rows(xt_plane, xt_scales)
-        levels.extend(load_levels(t) for t in (1, 2))
+        xt_all = sb.tile([P, T], U32, name="xt_all", tag="xt_all")
+        nc.sync.dma_start(xt_all[:].bitcast(I32), xt_words[0].rearrange("p c t -> p (c t)").bitcast(I32))
+        levels.extend(load_levels(t) for t in (2, 3))
         slot_list = load_list(offs5, "slot_list")
-        levels.append(load_levels(3))
+        sa_sb = load_per_row(sa, "sa_sb")
         wb_codes = sb.tile([P, N], U32, name="wb_codes", align_bytes=64)
         nc.sync.dma_start(wb_codes[:].bitcast(I32), wb_words[0].rearrange("p c t -> p (c t)").bitcast(I32))
-        load_scale_rows(wb_plane, wb_scales)
+        for q in range(QUADRANTS):
+            nc.sync.dma_start(
+                wb_plane[:].bitcast(I32)[QUADRANT * q : QUADRANT * q + PACK, :],
+                wb_scales[0].bitcast(I32)[PACK * q : PACK * (q + 1), :],
+            )
         place_list = load_list(offs6, "place_list")
         page_list = load_list(offs7, "page_list")
 
+        so_sb = sb.tile([P, HALVES], F32, name="so_sb")
+        with nc.allow_non_contiguous_dma(reason="one weight for each partition and half of the output features"):
+            nc.sync.dma_start(so_sb[:], so.rearrange("(h p) one -> p (h one)", p=P))
+
+        spread_scale_rows(wt_plane, wt_rows)
         wt_picked = sb.tile([P, R], U16, name="wt_picked")
         nc.vector.tensor_copy(wt_picked[:], wt_all[:].indirect(wt_list[:]))
         wt_codes = sb.tile([P, PACK, P], U16, name="wt_codes", align_bytes=64)
@@ -110,6 +117,7 @@ def tile_list_gatedlevels_chosen_one_postedout_kernel(
         )
         wt_scale = sb.tile([P, PACK, P], U8, name="wt_scale", align_bytes=64)
         nc.vector.tensor_copy(wt_scale[:].rearrange("p t m -> p m t"), wt_plane[:].indirect(wt_list[:]))
+        spread_scale_rows(xt_plane, xt_rows)
         xt_codes = sb.tile([P, J], U32, name="xt_codes", align_bytes=64)
         nc.vector.tensor_copy(xt_codes[:], xt_all[:].indirect(xt_list[:]))
         xt_scale = sb.tile([P, J], U8, name="xt_scale", align_bytes=64)
@@ -126,7 +134,7 @@ def tile_list_gatedlevels_chosen_one_postedout_kernel(
             nc.vector.tensor_copy(rows[:], bank[:])
             a_rows.append(rows)
 
-        u1 = []
+        u1 = sb.tile([P, PACK, O], F32, name="u1", tag="xt_all")
         for t in range(PACK):
             gate = sb.tile([P, O], F32, name=f"gate{t}")
             nc.scalar.activation(
@@ -137,26 +145,24 @@ def tile_list_gatedlevels_chosen_one_postedout_kernel(
             nc.scalar.activation(
                 stepped[:], levels[t][:].indirect(step_list[:]), ACT.Copy, scale=st_sb[:, t : t + 1],
             )
-            gated = sb.tile([P, O], F32, name=f"gated{t}", tag="xt_plane" if t == 0 else f"gated{t}", align_bytes=64)
-            nc.vector.tensor_tensor(gated[:], stepped[:], gate[:], ALU.mult)
-            u1.append(gated)
+            nc.vector.tensor_tensor(u1[:, t, :], stepped[:], gate[:], ALU.mult)
 
         p_rows = [sb.tile([P, O], F32, name=f"p_rows{h}") for h in range(HALVES)]
         chosen = sb.tile([P, HALVES, PACK, HALF], F32, name="chosen", tag=f"levels{PACK - 1}")
         for half in range(HALVES):
             places = slice(half * HALF, (half + 1) * HALF)
             columns = slice(half * HALF // PER_COLUMN, (half + 1) * HALF // PER_COLUMN)
-            hid = sb.tile([P, PACK, HALF], BF16, name="hid")
             for t in range(PACK):
                 nc.scalar.activation(
                     chosen[:, half, t, :], a_rows[t][:].indirect(slot_list[:, columns]), ACT.Copy,
                     scale=sa_sb[:, t : t + 1],
                 )
-                nc.vector.tensor_tensor(hid[:, t, :], u1[t][:, places], chosen[:, half, t, :], ALU.max)
-            woven = sb.tile([P, HALF, PACK], BF16, name=f"woven{half}", align_bytes=64)
-            nc.vector.tensor_copy(
+            woven = sb.tile([P, HALF, PACK], BF16, name="woven", align_bytes=64)
+            nc.vector.tensor_tensor(
                 woven[:].rearrange("p (c i) t -> p c t i", i=4),
-                hid[:].rearrange("p t (c i) -> p c t i", i=4),
+                u1[:, :, places].rearrange("p t (c i) -> p c t i", i=4),
+                chosen[:, half].rearrange("p t (c i) -> p c t i", i=4),
+                ALU.max,
             )
             hid_codes = sb.tile([P, HALF], U32, name=f"hid_codes{half}", align_bytes=64)
             hid_scale = sb.tile([P, HALF], U8, name=f"hid_scale{half}", align_bytes=64)

@@ -67,6 +67,11 @@ def tile_list_gatedlevels_chosen_one_postedout_kernel(
             nc.sync.dma_start(tile[:], tb_slots[t])
             return tile
 
+        warm_in = sb.tile([P, 1], F32, name="warm_in")
+        nc.gpsimd.memset(warm_in[:], 0.0)
+        warm_out = sb.tile([P, 1], F32, name="warm_out")
+        nc.scalar.activation(warm_out[:], warm_in[:], ACT.Sigmoid)
+
         wt_plane = zeroed_plane(V, "wt_plane")
         xt_plane = zeroed_plane(T, "xt_plane")
         wb_plane = zeroed_plane(N, "wb_plane")

from contextlib import ExitStack

import concourse.mybir as mybir

K, T, J, R, V, X, O, N, U, E = 512, 1024, 256, 512, 1024, 1024, 256, 256, 128, 512
FLOPS = 2 * K * R * J + 2 * R * N * O

F32 = mybir.dt.float32
BF16 = mybir.dt.bfloat16
I32 = mybir.dt.int32
U32 = mybir.dt.uint32
U16 = mybir.dt.uint16
U8 = mybir.dt.uint8
E4M3 = mybir.dt.float8_e4m3fn_x4
E5M2 = mybir.dt.float8_e5m2_x4
E2M1 = mybir.dt.float4_e2m1fn_x4
ACT = mybir.ActivationFunctionType
ALU = mybir.AluOpType

P = 128
PACK = 4
QUADRANTS = 4
QUADRANT = 32
HALVES = 2
HALF = O // HALVES
PER_COLUMN = 16


def tile_list_gatedlevels_chosen_one_postedout_kernel(
    tc, xt_words, xt_scales, wt_words, wt_scales, tb, st, sa, sg, bg, wb_words, wb_scales, so,
    offs, offs2, offs3, offs4, offs5, offs6, offs7, out,
):
    nc = tc.nc
    with ExitStack() as ctx:
        sb = ctx.enter_context(tc.tile_pool(name="sb", bufs=1))
        psum = ctx.enter_context(tc.psum_pool(name="psum", bufs=1))

        def load_list(src, name):
            tile = sb.tile(list(src.shape), U16, name=name)
            nc.sync.dma_start(tile[:], src)
            return tile

        def zeroed_plane(width, name):
            plane = sb.tile([P, width], U8, name=name, tag=name, align_bytes=64)
            nc.vector.memset(plane[:].bitcast(I32), 0)
            return plane

        def load_scale_rows(src, name):
            width = src.shape[2] // 4
            rows = sb.tile([PACK, QUADRANTS, width], I32, name=name)
            nc.sync.dma_start(rows[:], src[0].bitcast(I32).rearrange("(q r) c -> r q c", r=PACK))
            return rows

        def spread_scale_rows(plane, rows):
            for q in range(QUADRANTS):
                nc.vector.tensor_copy(plane[:].bitcast(I32)[QUADRANT * q : QUADRANT * q + PACK, :], rows[:, q, :])

        def load_per_row(src, name):
            tile = sb.tile([P, PACK], F32, name=name)
            nc.sync.dma_start(tile[:], src.rearrange("(p t) one -> p (t one)", t=PACK))
            return tile

        tb_slots = tb.rearrange("(p t) x -> t p x", t=PACK)

        def load_levels(t):
            tile = sb.tile([P, X], F32, name=f"levels{t}", tag=f"levels{t}")
            nc.sync.dma_start(tile[:], tb_slots[t])
            return tile

        warm_in = sb.tile([P, 1], F32, name="warm_in")
        nc.gpsimd.memset(warm_in[:], 0.0)
        warm_out = sb.tile([P, 1], F32, name="warm_out")
        nc.scalar.activation(warm_out[:], warm_in[:], ACT.Sigmoid)

        wt_plane = zeroed_plane(V, "wt_plane")
        xt_plane = zeroed_plane(T, "xt_plane")
        wb_plane = zeroed_plane(N, "wb_plane")
        pages = []
        for h in range(HALVES):
            page = sb.tile([P, E], F32, name=f"page{h}")
            nc.gpsimd.memset(page[:], 0.0)
            pages.append(page)

        wt_list = load_list(offs, "wt_list")
        wt_rows = load_scale_rows(wt_scales, "wt_rows")
        wt_all = sb.tile([P, V], U16, name="wt_all")
        nc.sync.dma_start(wt_all[:].bitcast(I32), wt_words[0].bitcast(I32))
        gate_list = load_list(offs4, "gate_list")
        sg_sb = load_per_row(sg, "sg_sb")
        bg_sb = load_per_row(bg, "bg_sb")
        levels = [load_levels(t) for t in (0, 1)]
        step_list = load_list(offs3, "step_list")
        st_sb = load_per_row(st, "st_sb")
        xt_rows = load_scale_rows(xt_scales, "xt_rows")
        xt_list = load_list(offs2, "xt_list")
        xt_all = sb.tile([P, T], U32, name="xt_all", tag="xt_all")
        nc.sync.dma_start(xt_all[:].bitcast(I32), xt_words[0].rearrange("p c t -> p (c t)").bitcast(I32))
        levels.extend(load_levels(t) for t in (2, 3))
        slot_list = load_list(offs5, "slot_list")
        sa_sb = load_per_row(sa, "sa_sb")
        wb_codes = sb.tile([P, N], U32, name="wb_codes", align_bytes=64)
        nc.sync.dma_start(wb_codes[:].bitcast(I32), wb_words[0].rearrange("p c t -> p (c t)").bitcast(I32))
        for q in range(QUADRANTS):
            nc.sync.dma_start(
                wb_plane[:].bitcast(I32)[QUADRANT * q : QUADRANT * q + PACK, :],
                wb_scales[0].bitcast(I32)[PACK * q : PACK * (q + 1), :],
            )
        place_list = load_list(offs6, "place_list")
        page_list = load_list(offs7, "page_list")

        so_sb = sb.tile([P, HALVES], F32, name="so_sb")
        with nc.allow_non_contiguous_dma(reason="one weight for each partition and half of the output features"):
            nc.sync.dma_start(so_sb[:], so.rearrange("(h p) one -> p (h one)", p=P))

        spread_scale_rows(wt_plane, wt_rows)
        wt_picked = sb.tile([P, R], U16, name="wt_picked")
        nc.vector.tensor_copy(wt_picked[:], wt_all[:].indirect(wt_list[:]))
        wt_codes = sb.tile([P, PACK, P], U16, name="wt_codes", align_bytes=64)
        nc.vector.tensor_copy(
            wt_codes[:].rearrange("p t (c i) -> p c t i", i=8),
            wt_picked[:].rearrange("p (c i t) -> p c t i", i=8, t=PACK),
        )
        wt_scale = sb.tile([P, PACK, P], U8, name="wt_scale", align_bytes=64)
        nc.vector.tensor_copy(wt_scale[:].rearrange("p t m -> p m t"), wt_plane[:].indirect(wt_list[:]))
        spread_scale_rows(xt_plane, xt_rows)
        xt_codes = sb.tile([P, J], U32, name="xt_codes", align_bytes=64)
        nc.vector.tensor_copy(xt_codes[:], xt_all[:].indirect(xt_list[:]))
        xt_scale = sb.tile([P, J], U8, name="xt_scale", align_bytes=64)
        nc.vector.tensor_copy(xt_scale[:], xt_plane[:].indirect(xt_list[:]))

        a_rows = []
        for t in range(PACK):
            bank = psum.tile([P, J], F32, name=f"a_bank{t}")
            nc.tensor.matmul_mx(
                out=bank[:], lhsT=wt_codes[:, t, :].bitcast(E2M1), lhsT_scale=wt_scale[:, t, :],
                rhs=xt_codes[:].bitcast(E4M3), rhs_scale=xt_scale[:], start=True, stop=True,
            )
            rows = sb.tile([P, J], F32, name=f"a_rows{t}")
            nc.vector.tensor_copy(rows[:], bank[:])
            a_rows.append(rows)

        u1 = sb.tile([P, PACK, O], F32, name="u1", tag="xt_all")
        for t in range(PACK):
            gate = sb.tile([P, O], F32, name=f"gate{t}")
            nc.scalar.activation(
                gate[:], levels[t][:].indirect(gate_list[:]), ACT.Sigmoid,
                bias=bg_sb[:, t : t + 1], scale=sg_sb[:, t : t + 1],
            )
            stepped = sb.tile([P, O], F32, name=f"stepped{t}")
            nc.scalar.activation(
                stepped[:], levels[t][:].indirect(step_list[:]), ACT.Copy, scale=st_sb[:, t : t + 1],
            )
            nc.vector.tensor_tensor(u1[:, t, :], stepped[:], gate[:], ALU.mult)

        p_rows = [sb.tile([P, O], F32, name=f"p_rows{h}") for h in range(HALVES)]
        chosen = sb.tile([P, HALVES, PACK, HALF], F32, name="chosen", tag=f"levels{PACK - 1}")
        for half in range(HALVES):
            places = slice(half * HALF, (half + 1) * HALF)
            columns = slice(half * HALF // PER_COLUMN, (half + 1) * HALF // PER_COLUMN)
            for t in range(PACK):
                nc.scalar.activation(
                    chosen[:, half, t, :], a_rows[t][:].indirect(slot_list[:, columns]), ACT.Copy,
                    scale=sa_sb[:, t : t + 1],
                )
            woven = sb.tile([P, HALF, PACK], BF16, name="woven", align_bytes=64)
            nc.vector.tensor_tensor(
                woven[:].rearrange("p (c i) t -> p c t i", i=4),
                u1[:, :, places].rearrange("p t (c i) -> p c t i", i=4),
                chosen[:, half].rearrange("p t (c i) -> p c t i", i=4),
                ALU.max,
            )
            hid_codes = sb.tile([P, HALF], U32, name=f"hid_codes{half}", align_bytes=64)
            hid_scale = sb.tile([P, HALF], U8, name=f"hid_scale{half}", align_bytes=64)
            nc.vector.quantize_mx(
                out=hid_codes[:].bitcast(E4M3), scales=hid_scale[:], in_=woven[:].rearrange("p o t -> p (o t)"),
            )
            for h in range(HALVES):
                features = slice(h * P, (h + 1) * P)
                bank = psum.tile([P, HALF], F32, name=f"p_bank{half}_{h}")
                nc.tensor.matmul_mx(
                    out=bank[:], lhsT=wb_codes[:, features].bitcast(E5M2), lhsT_scale=wb_plane[:, features],
                    rhs=hid_codes[:].bitcast(E4M3), rhs_scale=hid_scale[:], start=True, stop=True,
                )
                if half == HALVES - 1 and h == 0:
                    nc.scalar.copy(p_rows[h][:, places], bank[:])
                else:
                    nc.vector.tensor_copy(p_rows[h][:, places], bank[:])

        for h in range(HALVES):
            ends = sb.tile([P, U], F32, name=f"ends{h}")
            nc.scalar.activation(
                ends[:], p_rows[h][:].indirect(place_list[:]), ACT.Copy, scale=so_sb[:, h : h + 1],
            )
            if h == 0:
                nc.vector.tensor_copy(pages[h][:].indirect(page_list[:]), ends[:])
                nc.sync.dma_start(out[h * P : (h + 1) * P, :], pages[h][:])
            else:
                nc.scalar.activation(pages[h][:].indirect(page_list[:]), ends[:], ACT.Copy)
                nc.scalar.dma_start(out[h * P : (h + 1) * P, :], pages[h][:])
